import numpy as np, ml_dtypes
CORES = [2,10,50,58,66,74,122]
N = 7
NP, TK = 2, 256
def setup_inputs(rng):
    return {"x": rng.standard_normal((N, 128, TK), dtype=np.float32).astype(ml_dtypes.bfloat16), "w1": (rng.standard_normal((N, 128, 128), dtype=np.float32) / 8).astype(ml_dtypes.bfloat16), "w2": (rng.standard_normal((N, 128, NP * 128), dtype=np.float32) / 8).astype(ml_dtypes.bfloat16)}
def setup_inputs_big(rng):
    d = setup_inputs(rng)
    for k in ("x", "w1", "w2"): d[k] = (d[k].astype(np.float32) * 1024.0).astype(d[k].dtype)
    return d
def setup_inputs_small(rng):
    d = setup_inputs(rng)
    for k in ("x", "w1", "w2"): d[k] = (d[k].astype(np.float32) * (1 / 1024.0)).astype(d[k].dtype)
    return d
def setup_inputs_apart(rng):
    d = setup_inputs(rng)
    f = (10.0 ** rng.permutation(np.linspace(-1.5, 1.5, N))).astype(np.float32).reshape(N, 1, 1)
    for k in ("x", "w1", "w2"): d[k] = (d[k].astype(np.float32) * f).astype(d[k].dtype)
    return d
def reference(x, w1, w2):
    X, W1, W2 = x.astype(np.float64), w1.astype(np.float64), w2.astype(np.float64)
    h = [np.maximum(W1[p].T @ X[p], 0.0) for p in range(NP)]
    y = np.full((N, 128, TK), np.nan)
    for q in range(NP, N):
        y[q] = sum(W2[q][:, 128 * p:128 * p + 128].T @ h[p] for p in range(NP))
    return {"y": y.astype(ml_dtypes.bfloat16 if x.dtype != np.float64 else np.float64)}

@@ -1,0 +1,91 @@
+from concourse.bass import DstId, RemoteDMATransfer
+from concourse.mybir import AluOpType
+
+NP = 2
+D = 128
+TK = 256
+
+SCRATCH = {
+    "xs": ("sbuf", [D, TK], "bfloat16"),
+    "w1s": ("sbuf", [D, D], "bfloat16"),
+    "zero": ("sbuf", [D, TK], "float32"),
+    "hs": ("sbuf", [D, TK], "bfloat16"),
+    "w2s": ("sbuf", [D, NP * D], "bfloat16"),
+    "hin0": ("sbuf", [D, TK], "bfloat16"),
+    "hin1": ("sbuf", [D, TK], "bfloat16"),
+    "ys": ("sbuf", [D, TK], "bfloat16"),
+    "ps": ("psum", [D, TK], "float32"),
+}
+SEMAPHORES = ["ld", "zs", "mm", "hr", "sent", "a0", "a1", "yr", "st"]
+
+
+def _bits(mask):
+    n = 0
+    while mask:
+        n += mask & 1
+        mask >>= 1
+    return n
+
+
+def _hops(topo, a, b):
+    ca, cb = topo.chip(a), topo.chip(b)
+    if ca == cb:
+        return 0
+    if topo.mates(ca, cb) or topo.same_plane(ca, cb):
+        return 1
+    return 2
+
+
+def rank_program(g, core, T, topo):
+    rank = T.rank_of(core)
+    if rank is None:
+        return
+    S = T.sem
+    pcores = list(T.cores[:NP])
+    qcores = list(T.cores[NP:])
+
+    if rank < NP:
+        g.sync.dma_start(T.xs[:], T.x[:]).then_inc(S.ld, 16)
+        g.scalar.dma_start(T.w1s[:], T.w1[:]).then_inc(S.ld, 16)
+        g.vector.memset(T.zero[:], 0.0).then_inc(S.zs, 1)
+
+        g.tensor.wait_ge(S.ld, 32)
+        g.tensor.matmul(T.ps[:], T.w1s[:], T.xs[:], start=True, stop=True).then_inc(S.mm, 1)
+
+        g.vector.wait_ge(S.zs, 1)
+        g.vector.wait_ge(S.mm, 1)
+        g.vector.tensor_tensor(T.hs[:], T.ps[:], T.zero[:], AluOpType.max).then_inc(S.hr, 1)
+
+        dests = sorted(qcores, key=lambda d: _hops(topo, core, d))
+        mask = topo.mask(core, dests[0])
+        for d in dests:
+            mask &= topo.mask(core, d)
+        land = T["hin%d" % rank]
+        ids = []
+        for d in dests:
+            rid, pid, _se = topo.addr(d)
+            ids.append(DstId(rid=rid, pnc=pid))
+        g.wait_ge(S.hr, 1)
+        g.remote_dma_fused(
+            [RemoteDMATransfer(dst_ids=ids, dma_engine_mask=mask, remote_sem=S["a%d" % rank],
+                               srcs=[T.hs[:]], dsts=[land[:] for _d in dests], alu_op=0)],
+            local_sem=S.sent)
+        g.wait_ge(S.sent, _bits(mask))
+        return
+
+    g.sync.dma_start(T.w2s[:], T.w2[:]).then_inc(S.ld, 16)
+    order = sorted(range(NP), key=lambda p: _hops(topo, pcores[p], core))
+    g.tensor.wait_ge(S.ld, 16)
+    for i, p in enumerate(order):
+        n = _bits(topo.mask(pcores[p], core))
+        g.tensor.wait_ge(S["a%d" % p], n)
+        mmul = g.tensor.matmul(T.ps[:], T.w2s[:, D * p:D * p + D], T["hin%d" % p][:],
+                               start=(i == 0), stop=(i == NP - 1))
+    mmul.then_inc(S.mm, 1)
+
+    g.vector.wait_ge(S.mm, 1)
+    g.vector.tensor_copy(T.ys[:], T.ps[:]).then_inc(S.yr, 1)
+
+    g.sync.wait_ge(S.yr, 1)
+    g.sync.dma_start(T.y[:], T.ys[:]).then_inc(S.st, 16)
+    g.sync.wait_ge(S.st, 16)

@@ -4,19 +4,24 @@ from concourse.mybir import AluOpType
 NP = 2
 D = 128
 TK = 256
+HK = TK // 2
+BANK = 512
 
 SCRATCH = {
-    "xs": ("sbuf", [D, TK], "bfloat16"),
-    "w1s": ("sbuf", [D, D], "bfloat16"),
+    "xw": ("sbuf", [D, TK + D], "bfloat16"),
+    "xwin0": ("sbuf", [D, TK + D], "bfloat16"),
+    "xwin1": ("sbuf", [D, TK + D], "bfloat16"),
     "zero": ("sbuf", [D, TK], "float32"),
     "hs": ("sbuf", [D, TK], "bfloat16"),
     "w2s": ("sbuf", [D, NP * D], "bfloat16"),
     "hin0": ("sbuf", [D, TK], "bfloat16"),
     "hin1": ("sbuf", [D, TK], "bfloat16"),
     "ys": ("sbuf", [D, TK], "bfloat16"),
-    "ps": ("psum", [D, TK], "float32"),
+    "ph": ("psum", [D, BANK], "float32"),
+    "pa": ("psum", [D, BANK], "float32"),
+    "pb": ("psum", [D, BANK], "float32"),
 }
-SEMAPHORES = ["ld", "zs", "mm", "hr", "sent", "a0", "a1", "yr", "st"]
+SEMAPHORES = ["ld", "zs", "mh", "hr", "sent", "a0", "a1", "ma", "mb", "yr", "st"]
 
 
 def _bits(mask):
@@ -36,56 +41,87 @@ def _hops(topo, a, b):
     return 2
 
 
+def _plan(T, topo):
+    plan, taken = [], []
+    for p in range(NP):
+        dests = sorted(T.cores[NP:], key=lambda d: _hops(topo, T.cores[p], d))
+        first = [d for d in dests if d not in taken][0]
+        taken.append(first)
+        plan.append((first, [d for d in dests if d != first]))
+    return plan
+
+
+def _layer1(g, T, xw, h):
+    S = T.sem
+    g.tensor.matmul(T.ph[:, 0:TK], xw[:, TK:TK + D], xw[:, 0:TK], start=True, stop=True).then_inc(S.mh, 1)
+    g.vector.wait_ge(S.zs, 1)
+    g.vector.wait_ge(S.mh, 1)
+    g.vector.tensor_tensor(h[:], T.ph[:, 0:TK], T.zero[:], AluOpType.max).then_inc(S.hr, 1)
+
+
 def rank_program(g, core, T, topo):
     rank = T.rank_of(core)
     if rank is None:
         return
     S = T.sem
     pcores = list(T.cores[:NP])
-    qcores = list(T.cores[NP:])
+    plan = _plan(T, topo)
 
     if rank < NP:
-        g.sync.dma_start(T.xs[:], T.x[:]).then_inc(S.ld, 16)
-        g.scalar.dma_start(T.w1s[:], T.w1[:]).then_inc(S.ld, 16)
+        first, rest = plan[rank]
+        g.sync.dma_start(T.xw[:, 0:TK], T.x[:]).then_inc(S.ld, 16)
+        g.scalar.dma_start(T.xw[:, TK:TK + D], T.w1[:]).then_inc(S.ld, 16)
         g.vector.memset(T.zero[:], 0.0).then_inc(S.zs, 1)
 
-        g.tensor.wait_ge(S.ld, 32)
-        g.tensor.matmul(T.ps[:], T.w1s[:], T.xs[:], start=True, stop=True).then_inc(S.mm, 1)
-
-        g.vector.wait_ge(S.zs, 1)
-        g.vector.wait_ge(S.mm, 1)
-        g.vector.tensor_tensor(T.hs[:], T.ps[:], T.zero[:], AluOpType.max).then_inc(S.hr, 1)
-
-        dests = sorted(qcores, key=lambda d: _hops(topo, core, d))
-        mask = topo.mask(core, dests[0])
-        for d in dests:
+        mask = topo.mask(core, first)
+        for d in rest:
             mask &= topo.mask(core, d)
-        land = T["hin%d" % rank]
+        arrive = S["a%d" % rank]
+
+        g.wait_ge(S.ld, 32)
+        rid, pid, _se = topo.addr(first)
+        g.remote_dma(T["xwin%d" % rank][:], T.xw[:], arrive, S.sent, pid, rid, mask)
+
+        g.tensor.wait_ge(S.ld, 32)
+        _layer1(g, T, T.xw, T.hs)
+
         ids = []
-        for d in dests:
+        for d in rest:
             rid, pid, _se = topo.addr(d)
             ids.append(DstId(rid=rid, pnc=pid))
+        land = T["hin%d" % rank]
         g.wait_ge(S.hr, 1)
         g.remote_dma_fused(
-            [RemoteDMATransfer(dst_ids=ids, dma_engine_mask=mask, remote_sem=S["a%d" % rank],
-                               srcs=[T.hs[:]], dsts=[land[:] for _d in dests], alu_op=0)],
+            [RemoteDMATransfer(dst_ids=ids, dma_engine_mask=mask, remote_sem=arrive,
+                               srcs=[T.hs[:]], dsts=[land[:] for _d in rest], alu_op=0)],
             local_sem=S.sent)
-        g.wait_ge(S.sent, _bits(mask))
+        g.wait_ge(S.sent, 2 * _bits(mask))
         return
 
     g.sync.dma_start(T.w2s[:], T.w2[:]).then_inc(S.ld, 16)
-    order = sorted(range(NP), key=lambda p: _hops(topo, pcores[p], core))
+    raw = [p for p in range(NP) if plan[p][0] == core]
+    if raw:
+        g.vector.memset(T.zero[:], 0.0).then_inc(S.zs, 1)
+    order = sorted(range(NP), key=lambda p: (p not in raw, _hops(topo, pcores[p], core)))
     g.tensor.wait_ge(S.ld, 16)
     for i, p in enumerate(order):
-        n = _bits(topo.mask(pcores[p], core))
-        g.tensor.wait_ge(S["a%d" % p], n)
-        mmul = g.tensor.matmul(T.ps[:], T.w2s[:, D * p:D * p + D], T["hin%d" % p][:],
-                               start=(i == 0), stop=(i == NP - 1))
-    mmul.then_inc(S.mm, 1)
+        g.tensor.wait_ge(S["a%d" % p], _bits(topo.mask(pcores[p], core)))
+        h = T["hin%d" % p]
+        if p in raw:
+            _layer1(g, T, T["xwin%d" % p], h)
+            g.tensor.wait_ge(S.hr, 1)
+        w = T.w2s[:, D * p:D * p + D]
+        last = (i == NP - 1)
+        ma = g.tensor.matmul(T.pa[:, 0:HK], w, h[:, 0:HK], start=(i == 0), stop=last)
+        mb = g.tensor.matmul(T.pb[:, 0:HK], w, h[:, HK:TK], start=(i == 0), stop=last)
+    ma.then_inc(S.ma, 1)
+    mb.then_inc(S.mb, 1)
 
-    g.vector.wait_ge(S.mm, 1)
-    g.vector.tensor_copy(T.ys[:], T.ps[:]).then_inc(S.yr, 1)
+    g.vector.wait_ge(S.ma, 1)
+    g.vector.tensor_copy(T.ys[:, 0:HK], T.pa[:, 0:HK]).then_inc(S.yr, 1)
+    g.vector.wait_ge(S.mb, 1)
+    g.vector.tensor_copy(T.ys[:, HK:TK], T.pb[:, 0:HK]).then_inc(S.yr, 1)
 
-    g.sync.wait_ge(S.yr, 1)
+    g.sync.wait_ge(S.yr, 2)
     g.sync.dma_start(T.y[:], T.ys[:]).then_inc(S.st, 16)
     g.sync.wait_ge(S.st, 16)

@@ -21,7 +21,7 @@ SCRATCH = {
     "pa": ("psum", [D, BANK], "float32"),
     "pb": ("psum", [D, BANK], "float32"),
 }
-SEMAPHORES = ["ld", "zs", "mh", "hr", "sent", "a0", "a1", "ma", "mb", "yr", "st"]
+SEMAPHORES = ["ld", "lw", "zs", "mh", "hr", "sent", "a0", "a1", "ma", "mb", "yr", "st"]
 
 
 def _bits(mask):
@@ -44,7 +44,7 @@ def _hops(topo, a, b):
 def _plan(T, topo):
     plan, taken = [], []
     for p in range(NP):
-        dests = sorted(T.cores[NP:], key=lambda d: _hops(topo, T.cores[p], d))
+        dests = sorted(T.cores[NP:], key=lambda d: -_hops(topo, T.cores[p], d))
         first = [d for d in dests if d not in taken][0]
         taken.append(first)
         plan.append((first, [d for d in dests if d != first]))
@@ -69,8 +69,8 @@ def rank_program(g, core, T, topo):
 
     if rank < NP:
         first, rest = plan[rank]
-        g.sync.dma_start(T.xw[:, 0:TK], T.x[:]).then_inc(S.ld, 16)
-        g.scalar.dma_start(T.xw[:, TK:TK + D], T.w1[:]).then_inc(S.ld, 16)
+        g.sync.dma_start(T.xw[:, TK:TK + D], T.w1[:]).then_inc(S.lw, 16)
+        g.scalar.dma_start(T.xw[:, 0:TK], T.x[:]).then_inc(S.ld, 16)
         g.vector.memset(T.zero[:], 0.0).then_inc(S.zs, 1)
 
         mask = topo.mask(core, first)
@@ -78,11 +78,15 @@ def rank_program(g, core, T, topo):
             mask &= topo.mask(core, d)
         arrive = S["a%d" % rank]
 
-        g.wait_ge(S.ld, 32)
         rid, pid, _se = topo.addr(first)
-        g.remote_dma(T["xwin%d" % rank][:], T.xw[:], arrive, S.sent, pid, rid, mask)
+        raw = T["xwin%d" % rank]
+        g.wait_ge(S.lw, 16)
+        g.remote_dma(raw[:, TK:TK + D], T.xw[:, TK:TK + D], arrive, S.sent, pid, rid, mask)
+        g.wait_ge(S.ld, 16)
+        g.remote_dma(raw[:, 0:TK], T.xw[:, 0:TK], arrive, S.sent, pid, rid, mask)
 
-        g.tensor.wait_ge(S.ld, 32)
+        g.tensor.wait_ge(S.lw, 16)
+        g.tensor.wait_ge(S.ld, 16)
         _layer1(g, T, T.xw, T.hs)
 
         ids = []
@@ -95,17 +99,17 @@ def rank_program(g, core, T, topo):
             [RemoteDMATransfer(dst_ids=ids, dma_engine_mask=mask, remote_sem=arrive,
                                srcs=[T.hs[:]], dsts=[land[:] for _d in rest], alu_op=0)],
             local_sem=S.sent)
-        g.wait_ge(S.sent, 2 * _bits(mask))
+        g.wait_ge(S.sent, 3 * _bits(mask))
         return
 
     g.sync.dma_start(T.w2s[:], T.w2[:]).then_inc(S.ld, 16)
     raw = [p for p in range(NP) if plan[p][0] == core]
     if raw:
         g.vector.memset(T.zero[:], 0.0).then_inc(S.zs, 1)
-    order = sorted(range(NP), key=lambda p: (p not in raw, _hops(topo, pcores[p], core)))
+    order = sorted(range(NP), key=lambda p: ([plan[p][0]] + plan[p][1]).index(core))
     g.tensor.wait_ge(S.ld, 16)
     for i, p in enumerate(order):
-        g.tensor.wait_ge(S["a%d" % p], _bits(topo.mask(pcores[p], core)))
+        g.tensor.wait_ge(S["a%d" % p], (2 if p in raw else 1) * _bits(topo.mask(pcores[p], core)))
         h = T["hin%d" % p]
         if p in raw:
             _layer1(g, T, T["xwin%d" % p], h)

from concourse.bass import DstId, RemoteDMATransfer
from concourse.mybir import AluOpType

NP = 2
D = 128
TK = 256
HK = TK // 2
BANK = 512

SCRATCH = {
    "xw": ("sbuf", [D, TK + D], "bfloat16"),
    "xwin0": ("sbuf", [D, TK + D], "bfloat16"),
    "xwin1": ("sbuf", [D, TK + D], "bfloat16"),
    "zero": ("sbuf", [D, TK], "float32"),
    "hs": ("sbuf", [D, TK], "bfloat16"),
    "w2s": ("sbuf", [D, NP * D], "bfloat16"),
    "hin0": ("sbuf", [D, TK], "bfloat16"),
    "hin1": ("sbuf", [D, TK], "bfloat16"),
    "ys": ("sbuf", [D, TK], "bfloat16"),
    "ph": ("psum", [D, BANK], "float32"),
    "pa": ("psum", [D, BANK], "float32"),
    "pb": ("psum", [D, BANK], "float32"),
}
SEMAPHORES = ["ld", "lw", "zs", "mh", "hr", "sent", "a0", "a1", "ma", "mb", "yr", "st"]


def _bits(mask):
    n = 0
    while mask:
        n += mask & 1
        mask >>= 1
    return n


def _hops(topo, a, b):
    ca, cb = topo.chip(a), topo.chip(b)
    if ca == cb:
        return 0
    if topo.mates(ca, cb) or topo.same_plane(ca, cb):
        return 1
    return 2


def _plan(T, topo):
    plan, taken = [], []
    for p in range(NP):
        dests = sorted(T.cores[NP:], key=lambda d: -_hops(topo, T.cores[p], d))
        first = [d for d in dests if d not in taken][0]
        taken.append(first)
        plan.append((first, [d for d in dests if d != first]))
    return plan


def _layer1(g, T, xw, h):
    S = T.sem
    g.tensor.matmul(T.ph[:, 0:TK], xw[:, TK:TK + D], xw[:, 0:TK], start=True, stop=True).then_inc(S.mh, 1)
    g.vector.wait_ge(S.zs, 1)
    g.vector.wait_ge(S.mh, 1)
    g.vector.tensor_tensor(h[:], T.ph[:, 0:TK], T.zero[:], AluOpType.max).then_inc(S.hr, 1)


def rank_program(g, core, T, topo):
    rank = T.rank_of(core)
    if rank is None:
        return
    S = T.sem
    pcores = list(T.cores[:NP])
    plan = _plan(T, topo)

    if rank < NP:
        first, rest = plan[rank]
        g.sync.dma_start(T.xw[:, TK:TK + D], T.w1[:]).then_inc(S.lw, 16)
        g.scalar.dma_start(T.xw[:, 0:TK], T.x[:]).then_inc(S.ld, 16)
        g.vector.memset(T.zero[:], 0.0).then_inc(S.zs, 1)

        mask = topo.mask(core, first)
        for d in rest:
            mask &= topo.mask(core, d)
        arrive = S["a%d" % rank]

        rid, pid, _se = topo.addr(first)
        raw = T["xwin%d" % rank]
        g.wait_ge(S.lw, 16)
        g.remote_dma(raw[:, TK:TK + D], T.xw[:, TK:TK + D], arrive, S.sent, pid, rid, mask)
        g.wait_ge(S.ld, 16)
        g.remote_dma(raw[:, 0:TK], T.xw[:, 0:TK], arrive, S.sent, pid, rid, mask)

        g.tensor.wait_ge(S.lw, 16)
        g.tensor.wait_ge(S.ld, 16)
        _layer1(g, T, T.xw, T.hs)

        ids = []
        for d in rest:
            rid, pid, _se = topo.addr(d)
            ids.append(DstId(rid=rid, pnc=pid))
        land = T["hin%d" % rank]
        g.wait_ge(S.hr, 1)
        g.remote_dma_fused(
            [RemoteDMATransfer(dst_ids=ids, dma_engine_mask=mask, remote_sem=arrive,
                               srcs=[T.hs[:]], dsts=[land[:] for _d in rest], alu_op=0)],
            local_sem=S.sent)
        g.wait_ge(S.sent, 3 * _bits(mask))
        return

    g.sync.dma_start(T.w2s[:], T.w2[:]).then_inc(S.ld, 16)
    raw = [p for p in range(NP) if plan[p][0] == core]
    if raw:
        g.vector.memset(T.zero[:], 0.0).then_inc(S.zs, 1)
    order = sorted(range(NP), key=lambda p: ([plan[p][0]] + plan[p][1]).index(core))
    g.tensor.wait_ge(S.ld, 16)
    for i, p in enumerate(order):
        g.tensor.wait_ge(S["a%d" % p], (2 if p in raw else 1) * _bits(topo.mask(pcores[p], core)))
        h = T["hin%d" % p]
        if p in raw:
            _layer1(g, T, T["xwin%d" % p], h)
            g.tensor.wait_ge(S.hr, 1)
        w = T.w2s[:, D * p:D * p + D]
        last = (i == NP - 1)
        ma = g.tensor.matmul(T.pa[:, 0:HK], w, h[:, 0:HK], start=(i == 0), stop=last)
        mb = g.tensor.matmul(T.pb[:, 0:HK], w, h[:, HK:TK], start=(i == 0), stop=last)
    ma.then_inc(S.ma, 1)
    mb.then_inc(S.mb, 1)

    g.vector.wait_ge(S.ma, 1)
    g.vector.tensor_copy(T.ys[:, 0:HK], T.pa[:, 0:HK]).then_inc(S.yr, 1)
    g.vector.wait_ge(S.mb, 1)
    g.vector.tensor_copy(T.ys[:, HK:TK], T.pb[:, 0:HK]).then_inc(S.yr, 1)

    g.sync.wait_ge(S.yr, 2)
    g.sync.dma_start(T.y[:], T.ys[:]).then_inc(S.st, 16)
    g.sync.wait_ge(S.st, 16)
